import numpy as np
import ml_dtypes


def mxq(x, axis, fmt="e4m3"):
    dtype, down = {"e4m3": (ml_dtypes.float8_e4m3fn, 7), "e5m2": (ml_dtypes.float8_e5m2, 14)}[fmt]
    v = np.moveaxis(np.asarray(x, np.float32).astype(ml_dtypes.bfloat16).astype(np.float64), axis, -1)
    blocks = v.reshape(v.shape[:-1] + (-1, 32))
    amax = np.abs(blocks).max(-1, keepdims=True)
    byte = np.maximum(np.where(amax > 0, np.frexp(amax)[1] - 1 + 127, 0) - down, 1)
    scale = np.exp2(byte - 127.0)
    codes = (blocks / scale).astype(np.float32).astype(dtype).astype(np.float64)
    return np.moveaxis((codes * scale).reshape(v.shape), -1, axis)


WIDE = False


def mx_kscale(k):
    if not WIDE:
        return np.ones(k)
    levels = np.array([10, -10, 5, -5, 0])
    if k % 512:
        return np.exp2(np.random.permutation(np.resize(levels, k // 32))).repeat(32)
    a = np.empty((k // 512, 16))
    for p in range(k // 512):
        a[p, :8] = np.random.permutation(np.resize(levels, 8))
        for g in range(8):
            far = levels[np.abs(levels - a[p, g]) >= 10]
            a[p, g + 8] = far[np.random.randint(len(far))]
    return np.exp2(a.ravel()).repeat(32)


def f64(x):
    return np.asarray(x).astype(np.float64)


def striped(idx):
    return np.tile(idx.reshape(-1, 16).T, (8, 1)).astype(np.uint16)


def unstriped(offs):
    return offs[:16].T.reshape(-1).astype(np.int64)


def striped8(idx):
    return np.concatenate([x.reshape(-1, 16).T for x in idx]).astype(np.uint16)


def runs(offs, k):
    lists = np.stack([offs[16 * r : 16 * r + 16].T.reshape(-1) for r in range(8)]).astype(np.int64)
    return lists[np.arange(k) % 512 // 64]


def pack_weight(w):
    k, n = w.shape
    w = f64(np.asarray(w, np.float32).astype(ml_dtypes.bfloat16)).reshape(k // 32, 32, n)
    amax = np.abs(w).max(1)
    byte = np.clip(np.where(amax > 0, np.frexp(amax)[1] - 1 + 127 - 7, 1), 1, 254)
    scaled = (w * np.exp2(127.0 - byte)[:, None, :]).reshape(k, n).astype(np.float32)
    words = np.ascontiguousarray(scaled.reshape(k // 512, 128, 4, n).transpose(0, 1, 3, 2)).astype(ml_dtypes.float8_e4m3fn).view(np.uint8)
    return words, np.ascontiguousarray(byte.astype(np.uint8).reshape(k // 512, 16, n))


def unpack_weight(words, scales):
    g, p, n, _ = words.shape
    vals = np.ascontiguousarray(words).view(ml_dtypes.float8_e4m3fn).astype(np.float64) * np.repeat(np.exp2(scales.astype(np.float64) - 127.0), 8, axis=1)[..., None]
    return vals.transpose(0, 1, 3, 2).reshape(g * 512, n)

def planes(y):
    n, m = y.shape
    v = y.astype(np.float32).astype(ml_dtypes.bfloat16).astype(np.float64).reshape(n // 32, 32, m)
    top = np.abs(v).max(1)
    byte = np.clip(np.where(top > 0, np.frexp(top)[1] - 1 + 127 - 7, 1), 1, 254)
    codes = (v * np.exp2(127.0 - byte)[:, None, :]).reshape(n, m).astype(np.float32).astype(ml_dtypes.float8_e4m3fn).view(np.uint8)
    words = codes.reshape(n // 512, 128, 4, m).transpose(0, 1, 3, 2)
    return np.ascontiguousarray(words), np.ascontiguousarray(byte.astype(np.uint8).reshape(n // 512, 16, m))


K, T, S, N, H = 512, 2048, 512, 512, 512


def setup_inputs():
    n = np.random.standard_normal
    s = mx_kscale(K)[:, None]
    u = mx_kscale(S)
    packed_xT = pack_weight(n((K, T)) * s)
    packed_w1 = pack_weight(n((S, N)) / np.sqrt(S) / u[:, None])
    return {
        "x_words": packed_xT[0],
        "x_scales": packed_xT[1],
        "wa": (n((K, H)) / np.sqrt(K) / s).astype(np.float32),
        "wb": (n((K, H)) / np.sqrt(K) / s).astype(np.float32),
        "gt": (np.random.uniform(0.5, 1.5, (S, 1)) * u[:, None]).astype(np.float32),
        "w1_words": packed_w1[0],
        "w1_scales": packed_w1[1],
        "offs": striped(np.random.permutation(T)[:S]),
        "two": striped(np.random.permutation(T)[:S]),
        "n1": striped8(np.stack([np.random.permutation(H) for _ in range(8)])),
        "n2": striped8(np.stack([np.random.permutation(H) for _ in range(8)])),
        "n3": striped8(np.stack([np.random.permutation(H) for _ in range(8)])),
        "n4": striped8(np.stack([np.random.permutation(H) for _ in range(8)])),
        "n5": striped8(np.stack([np.random.permutation(H) for _ in range(8)])),
    }


def reference(x_words, x_scales, wa, wb, gt, w1_words, w1_scales, offs, two, n1, n2, n3, n4, n5):
    xq = unpack_weight(x_words, x_scales)[:, unstriped(offs)]
    y = xq.T @ mxq(f64(wa), 0, "e4m3")
    x_two = unpack_weight(x_words, x_scales)[:, unstriped(two)]
    d = x_two.T @ mxq(f64(wb), 0, "e4m3")
    z = f64(gt) * (np.maximum(np.minimum(y - (0.5 * (y[np.arange(S)[:, None], runs(n1, S)])), d[np.arange(S)[:, None], runs(n2, S)]), d[np.arange(S)[:, None], runs(n3, S)]))
    h = unpack_weight(w1_words, w1_scales).T @ mxq(z, 0, "e4m3")
    out_0 = 0.75 * ((h - (h[np.arange(N)[:, None], runs(n4, N)])) * (h - (h[np.arange(N)[:, None], runs(n5, N)])))
    return (out_0,) + planes(out_0)

@@ -1,0 +1,232 @@
+from contextlib import ExitStack
+
+import concourse.mybir as mybir
+
+K, T, S, N, H = 512, 2048, 512, 512, 512
+FLOPS = 2 * (2 * S * K * H + S * N * H)
+
+F32 = mybir.dt.float32
+BF16 = mybir.dt.bfloat16
+I32 = mybir.dt.int32
+U32 = mybir.dt.uint32
+U16 = mybir.dt.uint16
+U8 = mybir.dt.uint8
+FP8X4 = mybir.dt.float8_e4m3fn_x4
+ALU = mybir.AluOpType
+COPY = mybir.ActivationFunctionType.Copy
+
+P = 128
+PACK = 4
+HALF = H // 2
+LINE = 4
+
+
+def tile_picked_twtclampbquad_none_po_kernel(
+    tc, x_words, x_scales, wa, wb, gt, w1_words, w1_scales, offs, two, n1, n2, n3, n4, n5, out_0, out_1, out_2
+):
+    nc = tc.nc
+    halves = [slice(0, HALF), slice(HALF, H)]
+    list_halves = [slice(0, HALF // 16), slice(HALF // 16, H // 16)]
+
+    with ExitStack() as ctx:
+        lists = ctx.enter_context(tc.tile_pool(name="lists", bufs=1))
+        keep = ctx.enter_context(tc.tile_pool(name="keep", bufs=1))
+        psum = ctx.enter_context(tc.psum_pool(name="psum", bufs=1))
+
+        def sb(name, shape, dtype):
+            return keep.tile(shape, dtype, name=name, align_bytes=64)
+
+        def load_list(name, src):
+            dst = lists.tile([P, S // 16], U16, name=name)
+            nc.sync.dma_start(dst[:], src)
+            return dst
+
+        def load_scale_rows(dst, src):
+            for q in range(4):
+                nc.sync.dma_start(dst[32 * q : 32 * q + 4, :].bitcast(I32), src[0, 4 * q : 4 * q + 4, :].bitcast(I32))
+
+        def load_weight(name, src):
+            raw = []
+            for u in range(2):
+                part = sb("%s_raw%d" % (name, u), [P, PACK, HALF], F32)
+                nc.sync.dma_start(part[:], src.rearrange("(p j) h -> p j h", j=PACK)[:, :, halves[u]])
+                raw.append(part)
+            return raw
+
+        def interleave(engine_copy, dst, src):
+            engine_copy(
+                dst.rearrange("p (c i) t -> p c t i", i=LINE),
+                src.rearrange("p t (c i) -> p c t i", i=LINE),
+            )
+
+        xs = sb("xs", [P, T], U8)
+        nc.vector.memset(xs[:].bitcast(I32), 0)
+        two_l = load_list("two_l", two)
+        offs_l = load_list("offs_l", offs)
+        load_scale_rows(xs, x_scales)
+        wb_raw = load_weight("wb", wb)
+        xw = sb("xw", [P, T], I32)
+        nc.sync.dma_start(xw[:], x_words[0].rearrange("p c r -> p (c r)").bitcast(I32))
+        n2_l = load_list("n2_l", n2)
+        n3_l = load_list("n3_l", n3)
+        wa_raw = load_weight("wa", wa)
+        n1_l = load_list("n1_l", n1)
+        gt_sb = sb("gt_sb", [P, PACK], F32)
+        nc.sync.dma_start(gt_sb[:], gt.rearrange("(p t) o -> p (t o)", t=PACK))
+        w1s = sb("w1s", [P, N], U8)
+        nc.vector.memset(w1s[:].bitcast(I32), 0)
+        load_scale_rows(w1s, w1_scales)
+        w1w = sb("w1w", [P, N], I32)
+        nc.sync.dma_start(w1w[:], w1_words[0].rearrange("p c r -> p (c r)").bitcast(I32))
+        n4_l = load_list("n4_l", n4)
+        n5_l = load_list("n5_l", n5)
+
+        win = [sb("win%d" % t, [P, 2 * H], F32) for t in range(PACK)]
+        for t in range(PACK):
+            nc.vector.memset(win[t][:, H:], 0.0)
+
+        picked_s = sb("picked_s", [P, 2, S], U8)
+        nc.vector.tensor_copy(picked_s[:, 0, :], xs[:].indirect(two_l[:]))
+        nc.vector.tensor_copy(picked_s[:, 1, :], xs[:].indirect(offs_l[:]))
+        dealt_s = sb("dealt_s", [P, 2, PACK, P], U8)
+        nc.vector.tensor_copy(dealt_s[:], picked_s[:].rearrange("p l (m t) -> p l t m", t=PACK))
+
+        def cast_weight(name, raw):
+            grouped = sb(name + "_bf", [P, H, PACK], BF16)
+            for u in range(2):
+                interleave(nc.scalar.copy, grouped[:, halves[u], :], raw[u][:])
+            return grouped
+
+        def quantize(codes, scales, grouped):
+            nc.vector.quantize_mx(
+                out=codes.bitcast(FP8X4), scales=scales, in_=grouped.rearrange("p c t -> p (c t)")
+            )
+
+        wb_bf = cast_weight("wb", wb_raw)
+        wb_q = sb("wb_q", [P, H], U32)
+        wb_s = sb("wb_s", [P, H], U8)
+        quantize(wb_q[:], wb_s[:], wb_bf[:])
+
+        two_w = sb("two_w", [P, PACK, P], U32)
+        nc.vector.tensor_copy(two_w[:].rearrange("p t m -> p m t"), xw[:].bitcast(U32).indirect(two_l[:]))
+        offs_w = sb("offs_w", [P, PACK, P], U32)
+        nc.vector.tensor_copy(offs_w[:].rearrange("p t m -> p m t"), xw[:].bitcast(U32).indirect(offs_l[:]))
+
+        def product(bank, lhs_w, lhs_s, rhs_w, rhs_s):
+            nc.tensor.matmul_mx(
+                out=bank, lhsT=lhs_w.bitcast(FP8X4), lhsT_scale=lhs_s, rhs=rhs_w.bitcast(FP8X4), rhs_scale=rhs_s,
+                start=True, stop=True,
+            )
+
+        d2 = sb("d2", [P, PACK, H], F32)
+        d3 = sb("d3", [P, PACK, H], F32)
+        for t in range(PACK):
+            bank = psum.tile([P, H], F32, name="d_bank%d" % t, tag="bank%d" % t)
+            product(bank[:], two_w[:, t, :], dealt_s[:, 0, t, :], wb_q[:], wb_s[:])
+            nc.scalar.copy(win[t][:, :H], bank[:])
+            if t == 0:
+                wa_bf = cast_weight("wa", wa_raw)
+
+        def gather_d(t):
+            nc.vector.tensor_copy(d2[:, t, :], win[t][:].indirect(n2_l[:]))
+            nc.vector.tensor_copy(d3[:, t, :], win[t][:].indirect(n3_l[:]))
+
+        gather_d(0)
+        gather_d(1)
+        wa_q = sb("wa_q", [P, H], U32)
+        wa_s = sb("wa_s", [P, H], U8)
+        quantize(wa_q[:], wa_s[:], wa_bf[:])
+        ywin = [sb("ywin%d" % t, [P, H], F32) for t in range(PACK)]
+        y2 = sb("y2", [P, PACK, H], F32)
+        for t in range(PACK):
+            bank = psum.tile([P, H], F32, name="y_bank%d" % t, tag="bank%d" % (PACK + t))
+            product(bank[:], offs_w[:, t, :], dealt_s[:, 1, t, :], wa_q[:], wa_s[:])
+            nc.scalar.copy(ywin[t][:], bank[:])
+            nc.scalar.activation(y2[:, t, :], bank[:], COPY, scale=2.0)
+        gather_d(2)
+        gather_d(3)
+
+        w1w_d = sb("w1w_d", [P, PACK, P], I32)
+        nc.vector.tensor_copy(w1w_d[:], w1w[:].rearrange("p (m t) -> p t m", t=PACK))
+        w1s_d = sb("w1s_d", [P, PACK, P], U8)
+        nc.vector.tensor_copy(w1s_d[:], w1s[:].rearrange("p (m t) -> p t m", t=PACK))
+
+        z_q = sb("z_q", [P, H], U32)
+        z_s = sb("z_s", [P, H], U8)
+        hp = sb("hp", [P, PACK, H], F32)
+        zmax = []
+        zi = []
+
+        def clamp(u):
+            cols = halves[u]
+            a2 = sb("a2_%d" % u, [P, PACK, HALF], F32)
+            for t in range(PACK):
+                nc.vector.tensor_tensor(
+                    a2[:, t, :], ywin[t][:].indirect(n1_l[:, list_halves[u]]), y2[:, t, cols], ALU.subtract
+                )
+            low = sb("low%d" % u, [P, PACK, HALF], F32)
+            nc.vector.scalar_tensor_tensor(low[:], a2[:], -0.5, d2[:, :, cols], ALU.mult, ALU.min)
+            top = sb("top%d" % u, [P, PACK, HALF], F32)
+            nc.vector.tensor_tensor(top[:], low[:], d3[:, :, cols], ALU.max)
+            return top
+
+        def second_product(u, grouped):
+            cols = halves[u]
+            quantize(z_q[:, cols], z_s[:, cols], grouped[:])
+            for t in range(PACK):
+                bank = psum.tile([P, HALF], F32, name="h_bank%d_%d" % (u, t), tag="bank%d" % (PACK * u + t))
+                product(bank[:], w1w_d[:, t, :], w1s_d[:, t, :], z_q[:, cols], z_s[:, cols])
+                nc.scalar.copy(win[t][:, cols], bank[:])
+                nc.scalar.copy(hp[:, t, cols], bank[:])
+
+        top0 = clamp(0)
+        z0 = sb("z0", [P, PACK, HALF], BF16)
+        for t in range(PACK):
+            nc.scalar.activation(z0[:, t, :], top0[:, t, :], COPY, scale=gt_sb[:, t : t + 1])
+        z0i = sb("z0i", [P, HALF, PACK], BF16)
+        interleave(nc.scalar.copy, z0i[:], z0[:])
+        top1 = clamp(1)
+        second_product(0, z0i)
+        z1i = sb("z1i", [P, HALF, PACK], BF16)
+        nc.vector.tensor_tensor(
+            z1i[:].rearrange("p (c i) t -> p c t i", i=LINE),
+            top1[:].rearrange("p t (c i) -> p c t i", i=LINE),
+            gt_sb[:].unsqueeze(1).unsqueeze(3).to_broadcast([P, HALF // LINE, PACK, LINE]),
+            ALU.mult,
+        )
+        second_product(1, z1i)
+
+        res = sb("res", [P, PACK, H], F32)
+        out_rows = out_0.rearrange("(p t) h -> p t h", t=PACK)
+        o_q = sb("o_q", [P, H], U32)
+        o_s = sb("o_s", [P, H], U8)
+        words_out = out_1[0].rearrange("p c r -> p (c r)").bitcast(I32)
+
+        def differences(name, t, cols, lcols):
+            width = cols.stop - cols.start
+            p4 = sb("p4_" + name, [P, width], F32)
+            p5 = sb("p5_" + name, [P, width], F32)
+            nc.vector.tensor_tensor(p4[:], win[t][:].indirect(n4_l[:, lcols]), hp[:, t, cols], ALU.subtract)
+            nc.vector.tensor_tensor(p5[:], win[t][:].indirect(n5_l[:, lcols]), hp[:, t, cols], ALU.subtract)
+            return p4, p5
+
+        def finish(t, cols, p4, p5):
+            nc.vector.scalar_tensor_tensor(res[:, t, cols], p4[:], 0.75, p5[:], ALU.mult, ALU.mult)
+            nc.sync.dma_start(out_rows[:, t, cols], res[:, t, cols])
+
+        steps = [(t, slice(0, H), slice(0, H // 16)) for t in range(PACK - 1)]
+        steps = steps + [(PACK - 1, halves[u], list_halves[u]) for u in range(2)]
+        for i, (t, cols, lcols) in enumerate(steps):
+            p4, p5 = differences(str(i), t, cols, lcols)
+            finish(t, cols, p4, p5)
+            if i == PACK - 1:
+                o0i = sb("o0i", [P, HALF, PACK], BF16)
+                interleave(nc.scalar.copy, o0i[:], res[:, :, halves[0]])
+        o1i = sb("o1i", [P, HALF, PACK], BF16)
+        interleave(nc.vector.tensor_copy, o1i[:], res[:, :, halves[1]])
+        for u, grouped in enumerate((o0i, o1i)):
+            quantize(o_q[:, halves[u]], o_s[:, halves[u]], grouped[:])
+            nc.sync.dma_start(words_out[:, halves[u]], o_q[:, halves[u]].bitcast(I32))
+        for q in range(4):
+            queue = nc.scalar if q % 2 else nc.sync
+            queue.dma_start(out_2[0, 4 * q : 4 * q + 4, :].bitcast(I32), o_s[32 * q : 32 * q + 4, :].bitcast(I32))

@@ -13,12 +13,14 @@ U16 = mybir.dt.uint16
 U8 = mybir.dt.uint8
 FP8X4 = mybir.dt.float8_e4m3fn_x4
 ALU = mybir.AluOpType
-COPY = mybir.ActivationFunctionType.Copy
+ACT = mybir.ActivationFunctionType
+COPY = ACT.Copy
 
 P = 128
 PACK = 4
 HALF = H // 2
 LINE = 4
+SPLIT = 168
 
 
 def tile_picked_twtclampbquad_none_po_kernel(
@@ -33,8 +35,8 @@ def tile_picked_twtclampbquad_none_po_kernel(
         keep = ctx.enter_context(tc.tile_pool(name="keep", bufs=1))
         psum = ctx.enter_context(tc.psum_pool(name="psum", bufs=1))
 
-        def sb(name, shape, dtype):
-            return keep.tile(shape, dtype, name=name, align_bytes=64)
+        def sb(name, shape, dtype, tag=None):
+            return keep.tile(shape, dtype, name=name, tag=tag or name, align_bytes=64)
 
         def load_list(name, src):
             dst = lists.tile([P, S // 16], U16, name=name)
@@ -45,13 +47,12 @@ def tile_picked_twtclampbquad_none_po_kernel(
             for q in range(4):
                 nc.sync.dma_start(dst[32 * q : 32 * q + 4, :].bitcast(I32), src[0, 4 * q : 4 * q + 4, :].bitcast(I32))
 
-        def load_weight(name, src):
-            raw = []
-            for u in range(2):
-                part = sb("%s_raw%d" % (name, u), [P, PACK, HALF], F32)
-                nc.sync.dma_start(part[:], src.rearrange("(p j) h -> p j h", j=PACK)[:, :, halves[u]])
-                raw.append(part)
-            return raw
+        win = [sb("win%d" % t, [P, 2 * H], F32) for t in range(PACK)]
+
+        def load_weight(tile, src, u):
+            part = tile[:].rearrange("p (j h) -> p j h", j=PACK)
+            nc.sync.dma_start(part, src.rearrange("(p j) h -> p j h", j=PACK)[:, :, halves[u]])
+            return part
 
         def interleave(engine_copy, dst, src):
             engine_copy(
@@ -60,41 +61,40 @@ def tile_picked_twtclampbquad_none_po_kernel(
             )
 
         xs = sb("xs", [P, T], U8)
-        nc.vector.memset(xs[:].bitcast(I32), 0)
+        nc.vector.memset(xs[:, : T // 2].bitcast(I32), 0)
+        nc.gpsimd.memset(xs[:, T // 2 :].bitcast(I32), 0)
         two_l = load_list("two_l", two)
+        wb_raw = [load_weight(win[0], wb, 0)]
         offs_l = load_list("offs_l", offs)
         load_scale_rows(xs, x_scales)
-        wb_raw = load_weight("wb", wb)
+        wb_raw.append(load_weight(win[1], wb, 1))
         xw = sb("xw", [P, T], I32)
         nc.sync.dma_start(xw[:], x_words[0].rearrange("p c r -> p (c r)").bitcast(I32))
-        n2_l = load_list("n2_l", n2)
-        n3_l = load_list("n3_l", n3)
-        wa_raw = load_weight("wa", wa)
-        n1_l = load_list("n1_l", n1)
         gt_sb = sb("gt_sb", [P, PACK], F32)
         nc.sync.dma_start(gt_sb[:], gt.rearrange("(p t) o -> p (t o)", t=PACK))
+        n2_l = load_list("n2_l", n2)
+        n3_l = load_list("n3_l", n3)
+        wa_raw = [load_weight(win[2], wa, 0)]
         w1s = sb("w1s", [P, N], U8)
         nc.vector.memset(w1s[:].bitcast(I32), 0)
         load_scale_rows(w1s, w1_scales)
         w1w = sb("w1w", [P, N], I32)
         nc.sync.dma_start(w1w[:], w1_words[0].rearrange("p c r -> p (c r)").bitcast(I32))
+        wa_raw.append(load_weight(win[3], wa, 1))
+        n1_l = load_list("n1_l", n1)
         n4_l = load_list("n4_l", n4)
         n5_l = load_list("n5_l", n5)
-
-        win = [sb("win%d" % t, [P, 2 * H], F32) for t in range(PACK)]
-        for t in range(PACK):
-            nc.vector.memset(win[t][:, H:], 0.0)
 
         picked_s = sb("picked_s", [P, 2, S], U8)
         nc.vector.tensor_copy(picked_s[:, 0, :], xs[:].indirect(two_l[:]))
         nc.vector.tensor_copy(picked_s[:, 1, :], xs[:].indirect(offs_l[:]))
         dealt_s = sb("dealt_s", [P, 2, PACK, P], U8)
-        nc.vector.tensor_copy(dealt_s[:], picked_s[:].rearrange("p l (m t) -> p l t m", t=PACK))
+        nc.vector.tensor_copy(dealt_s[:, 0], picked_s[:, 0, :].rearrange("p (m t) -> p t m", t=PACK))
 
         def cast_weight(name, raw):
             grouped = sb(name + "_bf", [P, H, PACK], BF16)
             for u in range(2):
-                interleave(nc.scalar.copy, grouped[:, halves[u], :], raw[u][:])
+                interleave(nc.scalar.copy, grouped[:, halves[u], :], raw[u])
             return grouped
 
         def quantize(codes, scales, grouped):
@@ -107,8 +107,16 @@ def tile_picked_twtclampbquad_none_po_kernel(
         wb_s = sb("wb_s", [P, H], U8)
         quantize(wb_q[:], wb_s[:], wb_bf[:])
 
+        size = sb("size", [P, PACK], F32)
+        size2 = sb("size2", [P, PACK], F32)
+        sign = sb("sign", [P, PACK], F32)
+        nc.scalar.activation(size[:], gt_sb[:], ACT.Abs)
+        nc.scalar.activation(size2[:], gt_sb[:], ACT.Abs, scale=2.0)
+        nc.scalar.activation(sign[:], gt_sb[:], ACT.Sign)
+
         two_w = sb("two_w", [P, PACK, P], U32)
         nc.vector.tensor_copy(two_w[:].rearrange("p t m -> p m t"), xw[:].bitcast(U32).indirect(two_l[:]))
+        nc.vector.tensor_copy(dealt_s[:, 1], picked_s[:, 1, :].rearrange("p (m t) -> p t m", t=PACK))
         offs_w = sb("offs_w", [P, PACK, P], U32)
         nc.vector.tensor_copy(offs_w[:].rearrange("p t m -> p m t"), xw[:].bitcast(U32).indirect(offs_l[:]))
 
@@ -118,14 +126,14 @@ def tile_picked_twtclampbquad_none_po_kernel(
                 start=True, stop=True,
             )
 
-        d2 = sb("d2", [P, PACK, H], F32)
-        d3 = sb("d3", [P, PACK, H], F32)
+        d2 = sb("d2", [P, PACK, H], BF16)
+        d3 = sb("d3", [P, PACK, H], BF16)
         for t in range(PACK):
+            if t == 2:
+                wa_bf = cast_weight("wa", wa_raw)
             bank = psum.tile([P, H], F32, name="d_bank%d" % t, tag="bank%d" % t)
             product(bank[:], two_w[:, t, :], dealt_s[:, 0, t, :], wb_q[:], wb_s[:])
-            nc.scalar.copy(win[t][:, :H], bank[:])
-            if t == 0:
-                wa_bf = cast_weight("wa", wa_raw)
+            nc.scalar.activation(win[t][:, :H], bank[:], COPY, scale=size[:, t : t + 1])
 
         def gather_d(t):
             nc.vector.tensor_copy(d2[:, t, :], win[t][:].indirect(n2_l[:]))
@@ -137,38 +145,54 @@ def tile_picked_twtclampbquad_none_po_kernel(
         wa_s = sb("wa_s", [P, H], U8)
         quantize(wa_q[:], wa_s[:], wa_bf[:])
         ywin = [sb("ywin%d" % t, [P, H], F32) for t in range(PACK)]
-        y2 = sb("y2", [P, PACK, H], F32)
+        chunks = [slice(0, HALF), slice(HALF, HALF + HALF // 2), slice(HALF + HALF // 2, H)]
+        widths = [c.stop - c.start for c in chunks]
+        y2 = [sb("y2_%d" % c, [P, PACK, widths[c]], F32) for c in range(3)]
+        y_banks = []
         for t in range(PACK):
             bank = psum.tile([P, H], F32, name="y_bank%d" % t, tag="bank%d" % (PACK + t))
             product(bank[:], offs_w[:, t, :], dealt_s[:, 1, t, :], wa_q[:], wa_s[:])
-            nc.scalar.copy(ywin[t][:], bank[:])
-            nc.scalar.activation(y2[:, t, :], bank[:], COPY, scale=2.0)
+            nc.scalar.activation(ywin[t][:], bank[:], COPY, scale=size[:, t : t + 1])
+            nc.scalar.activation(y2[0][:, t, :], bank[:, halves[0]], COPY, scale=size2[:, t : t + 1])
+            y_banks.append(bank)
         gather_d(2)
         gather_d(3)
 
         w1w_d = sb("w1w_d", [P, PACK, P], I32)
-        nc.vector.tensor_copy(w1w_d[:], w1w[:].rearrange("p (m t) -> p t m", t=PACK))
+        nc.gpsimd.tensor_copy(w1w_d[:], w1w[:].rearrange("p (m t) -> p t m", t=PACK))
         w1s_d = sb("w1s_d", [P, PACK, P], U8)
-        nc.vector.tensor_copy(w1s_d[:], w1s[:].rearrange("p (m t) -> p t m", t=PACK))
+        nc.gpsimd.tensor_copy(w1s_d[:], w1s[:].rearrange("p (m t) -> p t m", t=PACK))
 
         z_q = sb("z_q", [P, H], U32)
         z_s = sb("z_s", [P, H], U8)
         hp = sb("hp", [P, PACK, H], F32)
-        zmax = []
-        zi = []
 
-        def clamp(u):
-            cols = halves[u]
-            a2 = sb("a2_%d" % u, [P, PACK, HALF], F32)
+        a2 = [sb("a2_%d" % c, [P, PACK, widths[c]], F32) for c in range(3)]
+        a_bf = sb("a_bf", [P, PACK, HALF], BF16)
+        low = [sb("low%d" % c, [P, PACK, widths[c]], BF16) for c in range(3)]
+        top = [sb("top%d" % c, [P, PACK, widths[c]], BF16) for c in range(2)]
+        zi = [sb("z%di" % u, [P, HALF, PACK], BF16) for u in range(2)]
+
+        def gather_y(c, t):
+            lcols = slice(chunks[c].start // 16, chunks[c].stop // 16)
+            nc.vector.tensor_tensor(a2[c][:, t, :], ywin[t][:].indirect(n1_l[:, lcols]), y2[c][:, t, :], ALU.subtract)
+
+        def read_y2(c, t):
+            nc.scalar.activation(y2[c][:, t, :], y_banks[t][:, chunks[c]], COPY, scale=size2[:, t : t + 1])
+
+        def lower(c):
+            nc.vector.scalar_tensor_tensor(low[c][:], a2[c][:], -0.5, d2[:, :, chunks[c]], ALU.mult, ALU.min)
+
+        def upper(c):
+            nc.vector.tensor_tensor(top[c][:], low[c][:], d3[:, :, chunks[c]], ALU.max)
+
+        def sign_on_scalar(c, dst):
+            signed = sb("signed%d" % c, [P, PACK, widths[c]], BF16)
             for t in range(PACK):
-                nc.vector.tensor_tensor(
-                    a2[:, t, :], ywin[t][:].indirect(n1_l[:, list_halves[u]]), y2[:, t, cols], ALU.subtract
-                )
-            low = sb("low%d" % u, [P, PACK, HALF], F32)
-            nc.vector.scalar_tensor_tensor(low[:], a2[:], -0.5, d2[:, :, cols], ALU.mult, ALU.min)
-            top = sb("top%d" % u, [P, PACK, HALF], F32)
-            nc.vector.tensor_tensor(top[:], low[:], d3[:, :, cols], ALU.max)
-            return top
+                nc.scalar.activation(signed[:, t, :], top[c][:, t, :], COPY, scale=sign[:, t : t + 1])
+            interleave(nc.scalar.copy, dst, signed[:])
+
+        h_banks = {}
 
         def second_product(u, grouped):
             cols = halves[u]
@@ -176,25 +200,45 @@ def tile_picked_twtclampbquad_none_po_kernel(
             for t in range(PACK):
                 bank = psum.tile([P, HALF], F32, name="h_bank%d_%d" % (u, t), tag="bank%d" % (PACK * u + t))
                 product(bank[:], w1w_d[:, t, :], w1s_d[:, t, :], z_q[:, cols], z_s[:, cols])
-                nc.scalar.copy(win[t][:, cols], bank[:])
-                nc.scalar.copy(hp[:, t, cols], bank[:])
+                h_banks[u, t] = bank
 
-        top0 = clamp(0)
-        z0 = sb("z0", [P, PACK, HALF], BF16)
+        read_y2(1, 0)
         for t in range(PACK):
-            nc.scalar.activation(z0[:, t, :], top0[:, t, :], COPY, scale=gt_sb[:, t : t + 1])
-        z0i = sb("z0i", [P, HALF, PACK], BF16)
-        interleave(nc.scalar.copy, z0i[:], z0[:])
-        top1 = clamp(1)
-        second_product(0, z0i)
-        z1i = sb("z1i", [P, HALF, PACK], BF16)
+            gather_y(0, t)
+            nc.scalar.activation(a_bf[:, t, :], a2[0][:, t, :], COPY, scale=-0.5)
+        for t in range(1, PACK):
+            read_y2(1, t)
+        for t in range(PACK):
+            read_y2(2, t)
+        gather_y(1, 0)
+        nc.vector.tensor_tensor(low[0][:], a_bf[:], d2[:, :, chunks[0]], ALU.min)
+        gather_y(1, 1)
+        upper(0)
+        sign_on_scalar(0, zi[0][:])
+        gather_y(1, 2)
+        gather_y(1, 3)
+        gather_y(2, 0)
+        lower(1)
+        gather_y(2, 1)
+        upper(1)
+        sign_on_scalar(1, zi[1][:, : widths[1], :])
+        gather_y(2, 2)
+        gather_y(2, 3)
+        lower(2)
+        second_product(0, zi[0])
+        top.append(sb("top2", [P, PACK, widths[2]], BF16, tag="z0i"))
+        upper(2)
         nc.vector.tensor_tensor(
-            z1i[:].rearrange("p (c i) t -> p c t i", i=LINE),
-            top1[:].rearrange("p t (c i) -> p c t i", i=LINE),
-            gt_sb[:].unsqueeze(1).unsqueeze(3).to_broadcast([P, HALF // LINE, PACK, LINE]),
+            zi[1][:, widths[1] :, :].rearrange("p (c i) t -> p c t i", i=LINE),
+            top[2][:].rearrange("p t (c i) -> p c t i", i=LINE),
+            sign[:].unsqueeze(1).unsqueeze(3).to_broadcast([P, widths[2] // LINE, PACK, LINE]),
             ALU.mult,
         )
-        second_product(1, z1i)
+        second_product(1, zi[1])
+        for t in range(PACK):
+            for u in range(2):
+                nc.scalar.copy(win[t][:, halves[u]], h_banks[u, t][:])
+                nc.scalar.copy(hp[:, t, halves[u]], h_banks[u, t][:])
 
         res = sb("res", [P, PACK, H], F32)
         out_rows = out_0.rearrange("(p t) h -> p t h", t=PACK)
@@ -214,16 +258,18 @@ def tile_picked_twtclampbquad_none_po_kernel(
             nc.vector.scalar_tensor_tensor(res[:, t, cols], p4[:], 0.75, p5[:], ALU.mult, ALU.mult)
             nc.sync.dma_start(out_rows[:, t, cols], res[:, t, cols])
 
-        steps = [(t, slice(0, H), slice(0, H // 16)) for t in range(PACK - 1)]
+        steps = [(0, halves[u], list_halves[u]) for u in range(2)]
+        steps = steps + [(t, slice(0, H), slice(0, H // 16)) for t in range(1, PACK - 1)]
         steps = steps + [(PACK - 1, halves[u], list_halves[u]) for u in range(2)]
         for i, (t, cols, lcols) in enumerate(steps):
             p4, p5 = differences(str(i), t, cols, lcols)
             finish(t, cols, p4, p5)
-            if i == PACK - 1:
+            if i == len(steps) - 2:
                 o0i = sb("o0i", [P, HALF, PACK], BF16)
                 interleave(nc.scalar.copy, o0i[:], res[:, :, halves[0]])
         o1i = sb("o1i", [P, HALF, PACK], BF16)
-        interleave(nc.vector.tensor_copy, o1i[:], res[:, :, halves[1]])
+        interleave(nc.vector.tensor_copy, o1i[:, :SPLIT, :], res[:, :, HALF : HALF + SPLIT])
+        interleave(nc.scalar.copy, o1i[:, SPLIT:, :], res[:, :, HALF + SPLIT :])
         for u, grouped in enumerate((o0i, o1i)):
             quantize(o_q[:, halves[u]], o_s[:, halves[u]], grouped[:])
             nc.sync.dma_start(words_out[:, halves[u]], o_q[:, halves[u]].bitcast(I32))

@@ -169,7 +169,7 @@ def tile_picked_twtclampbquad_none_po_kernel(
 
         a2 = [sb("a2_%d" % c, [P, PACK, widths[c]], F32) for c in range(3)]
         a_bf = sb("a_bf", [P, PACK, HALF], BF16)
-        low = [sb("low%d" % c, [P, PACK, widths[c]], BF16) for c in range(3)]
+        low = [sb("low%d" % c, [P, PACK, widths[c]], BF16) for c in range(2)]
         top = [sb("top%d" % c, [P, PACK, widths[c]], BF16) for c in range(2)]
         zi = [sb("z%di" % u, [P, HALF, PACK], BF16) for u in range(2)]
 
@@ -192,15 +192,16 @@ def tile_picked_twtclampbquad_none_po_kernel(
                 nc.scalar.activation(signed[:, t, :], top[c][:, t, :], COPY, scale=sign[:, t : t + 1])
             interleave(nc.scalar.copy, dst, signed[:])
 
-        h_banks = {}
+        h_first = []
+        h_banks = [psum.tile([P, H], F32, name="h_bank%d" % t, tag="bank%d" % t) for t in range(1, PACK)]
 
         def second_product(u, grouped):
             cols = halves[u]
             quantize(z_q[:, cols], z_s[:, cols], grouped[:])
+            h_first.append(psum.tile([P, HALF], F32, name="h_first%d" % u, tag="bank%d" % (PACK * u)))
             for t in range(PACK):
-                bank = psum.tile([P, HALF], F32, name="h_bank%d_%d" % (u, t), tag="bank%d" % (PACK * u + t))
-                product(bank[:], w1w_d[:, t, :], w1s_d[:, t, :], z_q[:, cols], z_s[:, cols])
-                h_banks[u, t] = bank
+                part = h_first[u][:] if t == 0 else h_banks[t - 1][:, cols]
+                product(part, w1w_d[:, t, :], w1s_d[:, t, :], z_q[:, cols], z_s[:, cols])
 
         read_y2(1, 0)
         for t in range(PACK):
@@ -224,21 +225,31 @@ def tile_picked_twtclampbquad_none_po_kernel(
         sign_on_scalar(1, zi[1][:, : widths[1], :])
         gather_y(2, 2)
         gather_y(2, 3)
-        lower(2)
+        part = widths[2] // 2
+        parts = [slice(0, part), slice(part, 2 * part)]
+        low.append(sb("low2", [P, PACK, widths[2]], BF16))
+        for cols in parts:
+            whole = slice(chunks[2].start + cols.start, chunks[2].start + cols.stop)
+            nc.vector.scalar_tensor_tensor(low[2][:, :, cols], a2[2][:, :, cols], -0.5, d2[:, :, whole], ALU.mult, ALU.min)
         second_product(0, zi[0])
         top.append(sb("top2", [P, PACK, widths[2]], BF16, tag="z0i"))
-        upper(2)
-        nc.vector.tensor_tensor(
-            zi[1][:, widths[1] :, :].rearrange("p (c i) t -> p c t i", i=LINE),
-            top[2][:].rearrange("p t (c i) -> p c t i", i=LINE),
-            sign[:].unsqueeze(1).unsqueeze(3).to_broadcast([P, widths[2] // LINE, PACK, LINE]),
-            ALU.mult,
-        )
+        for cols in parts:
+            whole = slice(chunks[2].start + cols.start, chunks[2].start + cols.stop)
+            nc.vector.tensor_tensor(top[2][:, :, cols], low[2][:, :, cols], d3[:, :, whole], ALU.max)
+        for cols in parts:
+            nc.vector.tensor_tensor(
+                zi[1][:, widths[1] + cols.start : widths[1] + cols.stop, :].rearrange("p (c i) t -> p c t i", i=LINE),
+                top[2][:, :, cols].rearrange("p t (c i) -> p c t i", i=LINE),
+                sign[:].unsqueeze(1).unsqueeze(3).to_broadcast([P, part // LINE, PACK, LINE]),
+                ALU.mult,
+            )
         second_product(1, zi[1])
-        for t in range(PACK):
-            for u in range(2):
-                nc.scalar.copy(win[t][:, halves[u]], h_banks[u, t][:])
-                nc.scalar.copy(hp[:, t, halves[u]], h_banks[u, t][:])
+        for u in range(2):
+            nc.scalar.copy(win[0][:, halves[u]], h_first[u][:])
+            nc.scalar.copy(hp[:, 0, halves[u]], h_first[u][:])
+        for t in range(1, PACK):
+            nc.scalar.copy(win[t][:, :H], h_banks[t - 1][:])
+            nc.scalar.copy(hp[:, t, :], h_banks[t - 1][:])
 
         res = sb("res", [P, PACK, H], F32)
         out_rows = out_0.rearrange("(p t) h -> p t h", t=PACK)
@@ -246,28 +257,32 @@ def tile_picked_twtclampbquad_none_po_kernel(
         o_s = sb("o_s", [P, H], U8)
         words_out = out_1[0].rearrange("p c r -> p (c r)").bitcast(I32)
 
-        def differences(name, t, cols, lcols):
-            width = cols.stop - cols.start
-            p4 = sb("p4_" + name, [P, width], F32)
-            p5 = sb("p5_" + name, [P, width], F32)
-            nc.vector.tensor_tensor(p4[:], win[t][:].indirect(n4_l[:, lcols]), hp[:, t, cols], ALU.subtract)
-            nc.vector.tensor_tensor(p5[:], win[t][:].indirect(n5_l[:, lcols]), hp[:, t, cols], ALU.subtract)
-            return p4, p5
+        steps = [(0, halves[u]) for u in range(2)]
+        steps = steps + [(t, slice(0, H)) for t in range(1, PACK - 1)]
+        steps = steps + [(PACK - 1, halves[u]) for u in range(2)]
+        p4 = sb("p4", [P, PACK, H], F32)
+        p5 = sb("p5", [P, PACK, H], F32)
 
-        def finish(t, cols, p4, p5):
-            nc.vector.scalar_tensor_tensor(res[:, t, cols], p4[:], 0.75, p5[:], ALU.mult, ALU.mult)
-            nc.sync.dma_start(out_rows[:, t, cols], res[:, t, cols])
+        def difference(dst, offsets, t, cols):
+            lcols = slice(cols.start // 16, cols.stop // 16)
+            nc.vector.tensor_tensor(dst[:, t, cols], win[t][:].indirect(offsets[:, lcols]), hp[:, t, cols], ALU.subtract)
 
-        steps = [(0, halves[u], list_halves[u]) for u in range(2)]
-        steps = steps + [(t, slice(0, H), slice(0, H // 16)) for t in range(1, PACK - 1)]
-        steps = steps + [(PACK - 1, halves[u], list_halves[u]) for u in range(2)]
-        for i, (t, cols, lcols) in enumerate(steps):
-            p4, p5 = differences(str(i), t, cols, lcols)
-            finish(t, cols, p4, p5)
-            if i == len(steps) - 2:
-                o0i = sb("o0i", [P, HALF, PACK], BF16)
-                interleave(nc.scalar.copy, o0i[:], res[:, :, halves[0]])
+        def multiply(t, cols):
+            nc.vector.scalar_tensor_tensor(res[:, t, cols], p4[:, t, cols], 0.75, p5[:, t, cols], ALU.mult, ALU.mult)
+
+        o0i = sb("o0i", [P, HALF, PACK], BF16)
         o1i = sb("o1i", [P, HALF, PACK], BF16)
+        for i, (t, cols) in enumerate(steps):
+            difference(p4, n4_l, t, cols)
+            if i > 0:
+                before, before_cols = steps[i - 1]
+                multiply(before, before_cols)
+                nc.sync.dma_start(out_rows[:, before, before_cols], res[:, before, before_cols])
+            difference(p5, n5_l, t, cols)
+        interleave(nc.scalar.copy, o0i[:], res[:, :, halves[0]])
+        multiply(PACK - 1, slice(HALF, HALF + SPLIT))
+        multiply(PACK - 1, slice(HALF + SPLIT, H))
+        nc.sync.dma_start(out_rows[:, PACK - 1, halves[1]], res[:, PACK - 1, halves[1]])
         interleave(nc.vector.tensor_copy, o1i[:, :SPLIT, :], res[:, :, HALF : HALF + SPLIT])
         interleave(nc.scalar.copy, o1i[:, SPLIT:, :], res[:, :, HALF + SPLIT :])
         for u, grouped in enumerate((o0i, o1i)):

from contextlib import ExitStack

import concourse.mybir as mybir

K, T, S, N, H = 512, 2048, 512, 512, 512
FLOPS = 2 * (2 * S * K * H + S * N * H)

F32 = mybir.dt.float32
BF16 = mybir.dt.bfloat16
I32 = mybir.dt.int32
U32 = mybir.dt.uint32
U16 = mybir.dt.uint16
U8 = mybir.dt.uint8
FP8X4 = mybir.dt.float8_e4m3fn_x4
ALU = mybir.AluOpType
ACT = mybir.ActivationFunctionType
COPY = ACT.Copy

P = 128
PACK = 4
HALF = H // 2
LINE = 4
SPLIT = 168


def tile_picked_twtclampbquad_none_po_kernel(
    tc, x_words, x_scales, wa, wb, gt, w1_words, w1_scales, offs, two, n1, n2, n3, n4, n5, out_0, out_1, out_2
):
    nc = tc.nc
    halves = [slice(0, HALF), slice(HALF, H)]
    list_halves = [slice(0, HALF // 16), slice(HALF // 16, H // 16)]

    with ExitStack() as ctx:
        lists = ctx.enter_context(tc.tile_pool(name="lists", bufs=1))
        keep = ctx.enter_context(tc.tile_pool(name="keep", bufs=1))
        psum = ctx.enter_context(tc.psum_pool(name="psum", bufs=1))

        def sb(name, shape, dtype, tag=None):
            return keep.tile(shape, dtype, name=name, tag=tag or name, align_bytes=64)

        def load_list(name, src):
            dst = lists.tile([P, S // 16], U16, name=name)
            nc.sync.dma_start(dst[:], src)
            return dst

        def load_scale_rows(dst, src):
            for q in range(4):
                nc.sync.dma_start(dst[32 * q : 32 * q + 4, :].bitcast(I32), src[0, 4 * q : 4 * q + 4, :].bitcast(I32))

        win = [sb("win%d" % t, [P, 2 * H], F32) for t in range(PACK)]

        def load_weight(tile, src, u):
            part = tile[:].rearrange("p (j h) -> p j h", j=PACK)
            nc.sync.dma_start(part, src.rearrange("(p j) h -> p j h", j=PACK)[:, :, halves[u]])
            return part

        def interleave(engine_copy, dst, src):
            engine_copy(
                dst.rearrange("p (c i) t -> p c t i", i=LINE),
                src.rearrange("p t (c i) -> p c t i", i=LINE),
            )

        xs = sb("xs", [P, T], U8)
        nc.vector.memset(xs[:, : T // 2].bitcast(I32), 0)
        nc.gpsimd.memset(xs[:, T // 2 :].bitcast(I32), 0)
        two_l = load_list("two_l", two)
        wb_raw = [load_weight(win[0], wb, 0)]
        offs_l = load_list("offs_l", offs)
        load_scale_rows(xs, x_scales)
        wb_raw.append(load_weight(win[1], wb, 1))
        xw = sb("xw", [P, T], I32)
        nc.sync.dma_start(xw[:], x_words[0].rearrange("p c r -> p (c r)").bitcast(I32))
        gt_sb = sb("gt_sb", [P, PACK], F32)
        nc.sync.dma_start(gt_sb[:], gt.rearrange("(p t) o -> p (t o)", t=PACK))
        n2_l = load_list("n2_l", n2)
        n3_l = load_list("n3_l", n3)
        wa_raw = [load_weight(win[2], wa, 0)]
        w1s = sb("w1s", [P, N], U8)
        nc.vector.memset(w1s[:].bitcast(I32), 0)
        load_scale_rows(w1s, w1_scales)
        w1w = sb("w1w", [P, N], I32)
        nc.sync.dma_start(w1w[:], w1_words[0].rearrange("p c r -> p (c r)").bitcast(I32))
        wa_raw.append(load_weight(win[3], wa, 1))
        n1_l = load_list("n1_l", n1)
        n4_l = load_list("n4_l", n4)
        n5_l = load_list("n5_l", n5)

        picked_s = sb("picked_s", [P, 2, S], U8)
        nc.vector.tensor_copy(picked_s[:, 0, :], xs[:].indirect(two_l[:]))
        nc.vector.tensor_copy(picked_s[:, 1, :], xs[:].indirect(offs_l[:]))
        dealt_s = sb("dealt_s", [P, 2, PACK, P], U8)
        nc.vector.tensor_copy(dealt_s[:, 0], picked_s[:, 0, :].rearrange("p (m t) -> p t m", t=PACK))

        def cast_weight(name, raw):
            grouped = sb(name + "_bf", [P, H, PACK], BF16)
            for u in range(2):
                interleave(nc.scalar.copy, grouped[:, halves[u], :], raw[u])
            return grouped

        def quantize(codes, scales, grouped):
            nc.vector.quantize_mx(
                out=codes.bitcast(FP8X4), scales=scales, in_=grouped.rearrange("p c t -> p (c t)")
            )

        wb_bf = cast_weight("wb", wb_raw)
        wb_q = sb("wb_q", [P, H], U32)
        wb_s = sb("wb_s", [P, H], U8)
        quantize(wb_q[:], wb_s[:], wb_bf[:])

        size = sb("size", [P, PACK], F32)
        size2 = sb("size2", [P, PACK], F32)
        sign = sb("sign", [P, PACK], F32)
        nc.scalar.activation(size[:], gt_sb[:], ACT.Abs)
        nc.scalar.activation(size2[:], gt_sb[:], ACT.Abs, scale=2.0)
        nc.scalar.activation(sign[:], gt_sb[:], ACT.Sign)

        two_w = sb("two_w", [P, PACK, P], U32)
        nc.vector.tensor_copy(two_w[:].rearrange("p t m -> p m t"), xw[:].bitcast(U32).indirect(two_l[:]))
        nc.vector.tensor_copy(dealt_s[:, 1], picked_s[:, 1, :].rearrange("p (m t) -> p t m", t=PACK))
        offs_w = sb("offs_w", [P, PACK, P], U32)
        nc.vector.tensor_copy(offs_w[:].rearrange("p t m -> p m t"), xw[:].bitcast(U32).indirect(offs_l[:]))

        def product(bank, lhs_w, lhs_s, rhs_w, rhs_s):
            nc.tensor.matmul_mx(
                out=bank, lhsT=lhs_w.bitcast(FP8X4), lhsT_scale=lhs_s, rhs=rhs_w.bitcast(FP8X4), rhs_scale=rhs_s,
                start=True, stop=True,
            )

        d2 = sb("d2", [P, PACK, H], BF16)
        d3 = sb("d3", [P, PACK, H], BF16)
        for t in range(PACK):
            if t == 2:
                wa_bf = cast_weight("wa", wa_raw)
            bank = psum.tile([P, H], F32, name="d_bank%d" % t, tag="bank%d" % t)
            product(bank[:], two_w[:, t, :], dealt_s[:, 0, t, :], wb_q[:], wb_s[:])
            nc.scalar.activation(win[t][:, :H], bank[:], COPY, scale=size[:, t : t + 1])

        def gather_d(t):
            nc.vector.tensor_copy(d2[:, t, :], win[t][:].indirect(n2_l[:]))
            nc.vector.tensor_copy(d3[:, t, :], win[t][:].indirect(n3_l[:]))

        gather_d(0)
        gather_d(1)
        wa_q = sb("wa_q", [P, H], U32)
        wa_s = sb("wa_s", [P, H], U8)
        quantize(wa_q[:], wa_s[:], wa_bf[:])
        ywin = [sb("ywin%d" % t, [P, H], F32) for t in range(PACK)]
        chunks = [slice(0, HALF), slice(HALF, HALF + HALF // 2), slice(HALF + HALF // 2, H)]
        widths = [c.stop - c.start for c in chunks]
        y2 = [sb("y2_%d" % c, [P, PACK, widths[c]], F32) for c in range(3)]
        y_banks = []
        for t in range(PACK):
            bank = psum.tile([P, H], F32, name="y_bank%d" % t, tag="bank%d" % (PACK + t))
            product(bank[:], offs_w[:, t, :], dealt_s[:, 1, t, :], wa_q[:], wa_s[:])
            nc.scalar.activation(ywin[t][:], bank[:], COPY, scale=size[:, t : t + 1])
            nc.scalar.activation(y2[0][:, t, :], bank[:, halves[0]], COPY, scale=size2[:, t : t + 1])
            y_banks.append(bank)
        gather_d(2)
        gather_d(3)

        w1w_d = sb("w1w_d", [P, PACK, P], I32)
        nc.gpsimd.tensor_copy(w1w_d[:], w1w[:].rearrange("p (m t) -> p t m", t=PACK))
        w1s_d = sb("w1s_d", [P, PACK, P], U8)
        nc.gpsimd.tensor_copy(w1s_d[:], w1s[:].rearrange("p (m t) -> p t m", t=PACK))

        z_q = sb("z_q", [P, H], U32)
        z_s = sb("z_s", [P, H], U8)
        hp = sb("hp", [P, PACK, H], F32)

        a2 = [sb("a2_%d" % c, [P, PACK, widths[c]], F32) for c in range(3)]
        a_bf = sb("a_bf", [P, PACK, HALF], BF16)
        low = [sb("low%d" % c, [P, PACK, widths[c]], BF16) for c in range(2)]
        top = [sb("top%d" % c, [P, PACK, widths[c]], BF16) for c in range(2)]
        zi = [sb("z%di" % u, [P, HALF, PACK], BF16) for u in range(2)]

        def gather_y(c, t):
            lcols = slice(chunks[c].start // 16, chunks[c].stop // 16)
            nc.vector.tensor_tensor(a2[c][:, t, :], ywin[t][:].indirect(n1_l[:, lcols]), y2[c][:, t, :], ALU.subtract)

        def read_y2(c, t):
            nc.scalar.activation(y2[c][:, t, :], y_banks[t][:, chunks[c]], COPY, scale=size2[:, t : t + 1])

        def lower(c):
            nc.vector.scalar_tensor_tensor(low[c][:], a2[c][:], -0.5, d2[:, :, chunks[c]], ALU.mult, ALU.min)

        def upper(c):
            nc.vector.tensor_tensor(top[c][:], low[c][:], d3[:, :, chunks[c]], ALU.max)

        def sign_on_scalar(c, dst):
            signed = sb("signed%d" % c, [P, PACK, widths[c]], BF16)
            for t in range(PACK):
                nc.scalar.activation(signed[:, t, :], top[c][:, t, :], COPY, scale=sign[:, t : t + 1])
            interleave(nc.scalar.copy, dst, signed[:])

        h_first = []
        h_banks = [psum.tile([P, H], F32, name="h_bank%d" % t, tag="bank%d" % t) for t in range(1, PACK)]

        def second_product(u, grouped):
            cols = halves[u]
            quantize(z_q[:, cols], z_s[:, cols], grouped[:])
            h_first.append(psum.tile([P, HALF], F32, name="h_first%d" % u, tag="bank%d" % (PACK * u)))
            for t in range(PACK):
                part = h_first[u][:] if t == 0 else h_banks[t - 1][:, cols]
                product(part, w1w_d[:, t, :], w1s_d[:, t, :], z_q[:, cols], z_s[:, cols])

        read_y2(1, 0)
        for t in range(PACK):
            gather_y(0, t)
            nc.scalar.activation(a_bf[:, t, :], a2[0][:, t, :], COPY, scale=-0.5)
        for t in range(1, PACK):
            read_y2(1, t)
        for t in range(PACK):
            read_y2(2, t)
        gather_y(1, 0)
        nc.vector.tensor_tensor(low[0][:], a_bf[:], d2[:, :, chunks[0]], ALU.min)
        gather_y(1, 1)
        upper(0)
        sign_on_scalar(0, zi[0][:])
        gather_y(1, 2)
        gather_y(1, 3)
        gather_y(2, 0)
        lower(1)
        gather_y(2, 1)
        upper(1)
        sign_on_scalar(1, zi[1][:, : widths[1], :])
        gather_y(2, 2)
        gather_y(2, 3)
        part = widths[2] // 2
        parts = [slice(0, part), slice(part, 2 * part)]
        low.append(sb("low2", [P, PACK, widths[2]], BF16))
        for cols in parts:
            whole = slice(chunks[2].start + cols.start, chunks[2].start + cols.stop)
            nc.vector.scalar_tensor_tensor(low[2][:, :, cols], a2[2][:, :, cols], -0.5, d2[:, :, whole], ALU.mult, ALU.min)
        second_product(0, zi[0])
        top.append(sb("top2", [P, PACK, widths[2]], BF16, tag="z0i"))
        for cols in parts:
            whole = slice(chunks[2].start + cols.start, chunks[2].start + cols.stop)
            nc.vector.tensor_tensor(top[2][:, :, cols], low[2][:, :, cols], d3[:, :, whole], ALU.max)
        for cols in parts:
            nc.vector.tensor_tensor(
                zi[1][:, widths[1] + cols.start : widths[1] + cols.stop, :].rearrange("p (c i) t -> p c t i", i=LINE),
                top[2][:, :, cols].rearrange("p t (c i) -> p c t i", i=LINE),
                sign[:].unsqueeze(1).unsqueeze(3).to_broadcast([P, part // LINE, PACK, LINE]),
                ALU.mult,
            )
        second_product(1, zi[1])
        for u in range(2):
            nc.scalar.copy(win[0][:, halves[u]], h_first[u][:])
            nc.scalar.copy(hp[:, 0, halves[u]], h_first[u][:])
        for t in range(1, PACK):
            nc.scalar.copy(win[t][:, :H], h_banks[t - 1][:])
            nc.scalar.copy(hp[:, t, :], h_banks[t - 1][:])

        res = sb("res", [P, PACK, H], F32)
        out_rows = out_0.rearrange("(p t) h -> p t h", t=PACK)
        o_q = sb("o_q", [P, H], U32)
        o_s = sb("o_s", [P, H], U8)
        words_out = out_1[0].rearrange("p c r -> p (c r)").bitcast(I32)

        steps = [(0, halves[u]) for u in range(2)]
        steps = steps + [(t, slice(0, H)) for t in range(1, PACK - 1)]
        steps = steps + [(PACK - 1, halves[u]) for u in range(2)]
        p4 = sb("p4", [P, PACK, H], F32)
        p5 = sb("p5", [P, PACK, H], F32)

        def difference(dst, offsets, t, cols):
            lcols = slice(cols.start // 16, cols.stop // 16)
            nc.vector.tensor_tensor(dst[:, t, cols], win[t][:].indirect(offsets[:, lcols]), hp[:, t, cols], ALU.subtract)

        def multiply(t, cols):
            nc.vector.scalar_tensor_tensor(res[:, t, cols], p4[:, t, cols], 0.75, p5[:, t, cols], ALU.mult, ALU.mult)

        o0i = sb("o0i", [P, HALF, PACK], BF16)
        o1i = sb("o1i", [P, HALF, PACK], BF16)
        for i, (t, cols) in enumerate(steps):
            difference(p4, n4_l, t, cols)
            if i > 0:
                before, before_cols = steps[i - 1]
                multiply(before, before_cols)
                nc.sync.dma_start(out_rows[:, before, before_cols], res[:, before, before_cols])
            difference(p5, n5_l, t, cols)
        interleave(nc.scalar.copy, o0i[:], res[:, :, halves[0]])
        multiply(PACK - 1, slice(HALF, HALF + SPLIT))
        multiply(PACK - 1, slice(HALF + SPLIT, H))
        nc.sync.dma_start(out_rows[:, PACK - 1, halves[1]], res[:, PACK - 1, halves[1]])
        interleave(nc.vector.tensor_copy, o1i[:, :SPLIT, :], res[:, :, HALF : HALF + SPLIT])
        interleave(nc.scalar.copy, o1i[:, SPLIT:, :], res[:, :, HALF + SPLIT :])
        for u, grouped in enumerate((o0i, o1i)):
            quantize(o_q[:, halves[u]], o_s[:, halves[u]], grouped[:])
            nc.sync.dma_start(words_out[:, halves[u]], o_q[:, halves[u]].bitcast(I32))
        for q in range(4):
            queue = nc.scalar if q % 2 else nc.sync
            queue.dma_start(out_2[0, 4 * q : 4 * q + 4, :].bitcast(I32), o_s[32 * q : 32 * q + 4, :].bitcast(I32))
